import numpy as np
CORES = [36,164,52,180,100,228,116,244]
N = 8
C = 512
SIGN = [[1,1,1,1,1,1,1,1],[1,-1,1,-1,1,-1,1,-1],[1,1,-1,-1,1,1,-1,-1],[1,-1,-1,1,1,-1,-1,1],[1,1,1,1,-1,-1,-1,-1],[1,-1,1,-1,-1,1,-1,1],[1,1,-1,-1,-1,-1,1,1],[1,-1,-1,1,-1,1,1,-1]]
def setup_inputs(rng):
    return {"x": rng.standard_normal((N, 128, C), dtype=np.float32), "w": (rng.standard_normal((N, 128, 128), dtype=np.float32) / 11)}
def setup_inputs_big(rng):
    d = setup_inputs(rng)
    for k in ("x", "w"): d[k] = (d[k].astype(np.float32) * 1024.0).astype(d[k].dtype)
    return d
def setup_inputs_small(rng):
    d = setup_inputs(rng)
    for k in ("x", "w"): d[k] = (d[k].astype(np.float32) * (1 / 1024.0)).astype(d[k].dtype)
    return d
def setup_inputs_apart(rng):
    d = setup_inputs(rng)
    f = (10.0 ** rng.permutation(np.linspace(-1.5, 1.5, N))).astype(np.float32).reshape(N, 1, 1)
    for k in ("x", "w"): d[k] = (d[k].astype(np.float32) * f).astype(d[k].dtype)
    return d
def reference(x, w):
    X = x.astype(np.float64)
    y = np.stack([w[r].astype(np.float64).T @ sum(SIGN[r][j] * X[j] for j in range(N)) for r in range(N)])
    return {"y": y.astype(np.float32)}

@@ -1,0 +1,139 @@
+from concourse.mybir import AluOpType
+
+C = 512
+HALF = 256
+STAGES = ((3, (1, 2, 3)), (4, (4,)))
+LAST = len(STAGES) - 1
+
+
+def _declare():
+    scratch = {
+        "ws": ("sbuf", [128, 128], "float32"),
+        "nw": ("sbuf", [128, 128], "float32"),
+        "zero": ("sbuf", [128, 128], "float32"),
+        "yo": ("sbuf", [128, C], "float32"),
+        "py0": ("psum", [128, C], "float32"),
+        "py1": ("psum", [128, C], "float32"),
+    }
+    sems = ["xl", "wl", "ls", "st", "zs", "nws", "m0", "m1", "c0", "c1"]
+    for s, (_, ds) in enumerate(STAGES):
+        scratch["v%d" % s] = ("sbuf", [128, C], "float32")
+        for d in ds:
+            scratch["l%d_%d" % (s, d)] = ("sbuf", [128, C], "float32")
+            sems.append("a%d_%d" % (s, d))
+        if s < LAST:
+            scratch["p%da" % s] = ("psum", [128, C], "float32")
+            scratch["p%db" % s] = ("psum", [128, C], "float32")
+            sems.append("q%d" % s)
+        if s > 0:
+            sems.append("r%d" % s)
+    return scratch, sems
+
+
+SCRATCH, SEMAPHORES = _declare()
+
+
+def _engines(mask):
+    return bin(mask).count("1")
+
+
+def rank_program(g, core, T, topo):
+    k = T.rank_of(core)
+    if k is None:
+        return
+    sign = T.tables["SIGN"]
+    S = T.sem
+    V = g.vector
+    P = g.tensor
+
+    def sg(s, j):
+        m = STAGES[s][0]
+        return sign[k & m][j & m]
+
+    def ready(q, s):
+        if s == 0:
+            q.wait_ge(S.xl, 16)
+        else:
+            q.wait_ge(S["r%d" % s], 1)
+
+    def n_arr(d):
+        return _engines(topo.mask(T.cores[k ^ d], core))
+
+    g.sync.dma_start(T.v0[:], T.x[:]).then_inc(S.xl, 16)
+    g.scalar.wait_ge(S.xl, 16)
+    g.scalar.dma_start(T.ws[:], T.w[:]).then_inc(S.wl, 16)
+
+    left = 0
+    for s, (_, ds) in enumerate(STAGES):
+        ready(g, s)
+        for d in ds:
+            dst = T.cores[k ^ d]
+            rid, pid = topo.addr(dst, core)
+            mask = topo.mask(core, dst)
+            g.remote_dma(out_ap=T["l%d_%d" % (s, d)][:], in_ap=T["v%d" % s][:], remote_sem=S["a%d_%d" % (s, d)],
+                         local_sem=S.ls, pid=pid, routing_id=rid, dma_engine_mask=mask)
+            left += _engines(mask)
+
+    last_ds = STAGES[LAST][1]
+    need_neg = min([sg(LAST, k)] + [sg(LAST, k ^ d) for d in last_ds]) < 0
+    if need_neg:
+        V.memset(T.zero[:], 0.0).then_inc(S.zs, 1)
+        V.wait_ge(S.zs, 1)
+        V.wait_ge(S.wl, 16)
+        V.tensor_tensor(T.nw[:], T.zero[:], T.ws[:], AluOpType.subtract).then_inc(S.nws, 1)
+
+    for s, (_, ds) in enumerate(STAGES[:LAST]):
+        q = S["q%d" % s]
+        banks = (T["p%da" % s], T["p%db" % s])
+        ready(V, s)
+        acc, sig, done = T["v%d" % s][:], sg(s, k), 0
+        if len(ds) == 1:
+            V.tensor_copy(banks[1][:], acc).then_inc(q, 1)
+            acc, done = banks[1][:], 1
+        for i, d in enumerate(ds):
+            new, tau = T["l%d_%d" % (s, d)][:], sg(s, k ^ d)
+            V.wait_ge(S["a%d_%d" % (s, d)], n_arr(d))
+            if done:
+                V.wait_ge(q, done)
+            final = i == len(ds) - 1
+            out = T["v%d" % (s + 1)][:] if final else banks[i % 2][:]
+            if sig == tau:
+                ins = V.tensor_tensor(out, acc, new, AluOpType.add)
+            elif sig > 0:
+                ins = V.tensor_tensor(out, acc, new, AluOpType.subtract)
+            else:
+                ins = V.tensor_tensor(out, new, acc, AluOpType.subtract)
+                sig = 1
+            if final:
+                ins.then_inc(S["r%d" % (s + 1)], 1)
+            else:
+                ins.then_inc(q, 1)
+                done += 1
+            acc = out
+        assert sig > 0
+
+    P.wait_ge(S.wl, 16)
+    if need_neg:
+        P.wait_ge(S.nws, 1)
+    ready(P, LAST)
+    terms = [(T["v%d" % LAST], sg(LAST, k), None)]
+    terms += [(T["l%d_%d" % (LAST, d)], sg(LAST, k ^ d), d) for d in last_ds]
+    for i, (buf, sig, d) in enumerate(terms):
+        if d is not None:
+            P.wait_ge(S["a%d_%d" % (LAST, d)], n_arr(d))
+        lhs = T.ws[:] if sig > 0 else T.nw[:]
+        for h in range(2):
+            ins = P.matmul(T["py%d" % h][:, 0:HALF], lhs, buf[:, h * HALF:(h + 1) * HALF],
+                           start=(i == 0), stop=(i == len(terms) - 1))
+            if i == len(terms) - 1:
+                ins.then_inc(S["m%d" % h], 1)
+
+    for h, q in enumerate((g.sync, g.scalar)):
+        cols = slice(h * HALF, (h + 1) * HALF)
+        V.wait_ge(S["m%d" % h], 1)
+        V.tensor_copy(T.yo[:, cols], T["py%d" % h][:, 0:HALF]).then_inc(S["c%d" % h], 1)
+        q.wait_ge(S["c%d" % h], 1)
+        q.dma_start(T.y[:, cols], T.yo[:, cols]).then_inc(S.st, 16)
+
+    g.wait_ge(S.ls, left)
+    g.wait_ge(S.st, 32)

@@ -1,40 +1,27 @@
+from concourse.bass import DstId, RemoteDMATransfer
 from concourse.mybir import AluOpType
 
-C = 512
-HALF = 256
-STAGES = ((3, (1, 2, 3)), (4, (4,)))
-LAST = len(STAGES) - 1
+N = 8
+CH = 64
+Q = 256
 
-
-def _declare():
-    scratch = {
-        "ws": ("sbuf", [128, 128], "float32"),
-        "nw": ("sbuf", [128, 128], "float32"),
-        "zero": ("sbuf", [128, 128], "float32"),
-        "yo": ("sbuf", [128, C], "float32"),
-        "py0": ("psum", [128, C], "float32"),
-        "py1": ("psum", [128, C], "float32"),
-    }
-    sems = ["xl", "wl", "ls", "st", "zs", "nws", "m0", "m1", "c0", "c1"]
-    for s, (_, ds) in enumerate(STAGES):
-        scratch["v%d" % s] = ("sbuf", [128, C], "float32")
-        for d in ds:
-            scratch["l%d_%d" % (s, d)] = ("sbuf", [128, C], "float32")
-            sems.append("a%d_%d" % (s, d))
-        if s < LAST:
-            scratch["p%da" % s] = ("psum", [128, C], "float32")
-            scratch["p%db" % s] = ("psum", [128, C], "float32")
-            sems.append("q%d" % s)
-        if s > 0:
-            sems.append("r%d" % s)
-    return scratch, sems
-
-
-SCRATCH, SEMAPHORES = _declare()
-
-
-def _engines(mask):
-    return bin(mask).count("1")
+SCRATCH = {
+    "xs": ("sbuf", [128, 512], "float32"),
+    "la": ("sbuf", [128, 512], "float32"),
+    "us0": ("sbuf", [128, 128], "float32"),
+    "us1": ("sbuf", [128, 128], "float32"),
+    "vf": ("sbuf", [128, 256], "float32"),
+    "ts": ("sbuf", [128, 512], "float32"),
+    "rs": ("sbuf", [128, 512], "float32"),
+    "ws": ("sbuf", [128, 128], "float32"),
+    "yo": ("sbuf", [128, 512], "float32"),
+    "pu0": ("psum", [128, 512], "float32"),
+    "pu1": ("psum", [128, 512], "float32"),
+    "pv": ("psum", [128, 512], "float32"),
+    "py0": ("psum", [128, 512], "float32"),
+    "py1": ("psum", [128, 512], "float32"),
+}
+SEMAPHORES = ["xn", "xf", "wl", "ls", "st", "a1", "a2", "a3", "a4", "dv", "tn", "tf", "ro", "m0", "m1", "c0", "c1"]
 
 
 def rank_program(g, core, T, topo):
@@ -45,95 +32,92 @@ def rank_program(g, core, T, topo):
     S = T.sem
     V = g.vector
     P = g.tensor
+    qn = k // 4
+    qf = 1 - qn
 
-    def sg(s, j):
-        m = STAGES[s][0]
-        return sign[k & m][j & m]
+    def ch(buf, j):
+        return buf[:, j * CH:(j + 1) * CH]
 
-    def ready(q, s):
-        if s == 0:
-            q.wait_ge(S.xl, 16)
-        else:
-            q.wait_ge(S["r%d" % s], 1)
+    def quad(buf, q):
+        return buf[:, q * Q:(q + 1) * Q]
 
-    def n_arr(d):
-        return _engines(topo.mask(T.cores[k ^ d], core))
+    def op(bit, out_bit):
+        return AluOpType.add if sign[bit * out_bit][bit] > 0 else AluOpType.subtract
 
-    g.sync.dma_start(T.v0[:], T.x[:]).then_inc(S.xl, 16)
-    g.scalar.wait_ge(S.xl, 16)
-    g.scalar.dma_start(T.ws[:], T.w[:]).then_inc(S.wl, 16)
+    near = [j for j in range(N) if j // 4 == qn and j != k]
+    far = [j for j in range(N) if j // 4 == qf]
 
-    left = 0
-    for s, (_, ds) in enumerate(STAGES):
-        ready(g, s)
-        for d in ds:
-            dst = T.cores[k ^ d]
-            rid, pid = topo.addr(dst, core)
-            mask = topo.mask(core, dst)
-            g.remote_dma(out_ap=T["l%d_%d" % (s, d)][:], in_ap=T["v%d" % s][:], remote_sem=S["a%d_%d" % (s, d)],
-                         local_sem=S.ls, pid=pid, routing_id=rid, dma_engine_mask=mask)
-            left += _engines(mask)
+    def per_transfer(dsts):
+        lists = []
+        for i, j in enumerate(dsts):
+            m = topo.mask(core, T.cores[j])
+            e = [b for b in range(16) if (m >> b) & 1]
+            lists.append((1 << e[2 * i]) | (1 << e[2 * i + 1]))
+        return lists
 
-    last_ds = STAGES[LAST][1]
-    need_neg = min([sg(LAST, k)] + [sg(LAST, k ^ d) for d in last_ds]) < 0
-    if need_neg:
-        V.memset(T.zero[:], 0.0).then_inc(S.zs, 1)
-        V.wait_ge(S.zs, 1)
-        V.wait_ge(S.wl, 16)
-        V.tensor_tensor(T.nw[:], T.zero[:], T.ws[:], AluOpType.subtract).then_inc(S.nws, 1)
+    left = [0]
 
-    for s, (_, ds) in enumerate(STAGES[:LAST]):
-        q = S["q%d" % s]
-        banks = (T["p%da" % s], T["p%db" % s])
-        ready(V, s)
-        acc, sig, done = T["v%d" % s][:], sg(s, k), 0
-        if len(ds) == 1:
-            V.tensor_copy(banks[1][:], acc).then_inc(q, 1)
-            acc, done = banks[1][:], 1
-        for i, d in enumerate(ds):
-            new, tau = T["l%d_%d" % (s, d)][:], sg(s, k ^ d)
-            V.wait_ge(S["a%d_%d" % (s, d)], n_arr(d))
-            if done:
-                V.wait_ge(q, done)
-            final = i == len(ds) - 1
-            out = T["v%d" % (s + 1)][:] if final else banks[i % 2][:]
-            if sig == tau:
-                ins = V.tensor_tensor(out, acc, new, AluOpType.add)
-            elif sig > 0:
-                ins = V.tensor_tensor(out, acc, new, AluOpType.subtract)
-            else:
-                ins = V.tensor_tensor(out, new, acc, AluOpType.subtract)
-                sig = 1
-            if final:
-                ins.then_inc(S["r%d" % (s + 1)], 1)
-            else:
-                ins.then_inc(q, 1)
-                done += 1
-            acc = out
-        assert sig > 0
+    def wave(dsts, src_buf, dst_buf, sem):
+        trs = []
+        for j, m in zip(dsts, per_transfer(dsts)):
+            rid, pid = topo.addr(T.cores[j], core)
+            trs.append(RemoteDMATransfer(dst_ids=[DstId(rid=rid, pnc=pid)], dma_engine_mask=m, remote_sem=sem,
+                                         src=ch(src_buf, j), dst=ch(dst_buf, k)))
+            left[0] += 2
+        g.remote_dma_fused(trs, local_sem=S.ls)
+
+    g.sync.dma_start(quad(T.xs, qn), quad(T.x, qn)).then_inc(S.xn, 16)
+    g.scalar.dma_start(quad(T.xs, qf), quad(T.x, qf)).then_inc(S.xf, 16)
+    g.sync.wait_ge(S.xf, 16)
+    g.sync.dma_start(T.ws[:], T.w[:]).then_inc(S.wl, 16)
+
+    g.wait_ge(S.xn, 16)
+    wave(near, T.xs, T.la, S.a1)
+    g.wait_ge(S.xf, 16)
+    wave(far, T.xs, T.la, S.a2)
+    g.wait_ge(S.tn, 1)
+    wave(near, T.ts, T.rs, S.a3)
+    g.wait_ge(S.tf, 1)
+    wave(far, T.ts, T.rs, S.a4)
+
+    done = [0]
+
+    def step(ins):
+        ins.then_inc(S.dv, 1)
+        done[0] += 1
+
+    def lower_stages(q, pu, us, out):
+        for b1, dst in ((0, pu), (1, us)):
+            a, b = ch(T.la, 4 * q + 2 * b1), ch(T.la, 4 * q + 2 * b1 + 1)
+            for r0 in range(2):
+                step(V.tensor_tensor(ch(dst, r0), a, b, op(1, r0)))
+        V.wait_ge(S.dv, done[0])
+        for r1 in range(2):
+            step(V.tensor_tensor(out[:, r1 * 128:(r1 + 1) * 128], pu[:, 0:128], us[:, 0:128], op(2, r1)))
+
+    V.wait_ge(S.xn, 16)
+    step(V.tensor_copy(ch(T.la, k), ch(T.xs, k)))
+    V.wait_ge(S.a1, 2 * len(near))
+    V.wait_ge(S.dv, done[0])
+    lower_stages(qn, T.pu0, T.us0, T.pv)
+    V.wait_ge(S.a2, 2 * len(far))
+    lower_stages(qf, T.pu1, T.us1, T.vf)
+    V.wait_ge(S.dv, done[0])
+    lo, hi = (T.pv[:, 0:Q], T.vf[:]) if qn == 0 else (T.vf[:], T.pv[:, 0:Q])
+    V.tensor_tensor(quad(T.ts, qn), lo, hi, op(4, qn)).then_inc(S.tn, 1)
+    V.tensor_tensor(quad(T.ts, qf), lo, hi, op(4, qf)).then_inc(S.tf, 1)
+    V.wait_ge(S.tn, 1)
+    V.tensor_copy(ch(T.rs, k), ch(T.ts, k)).then_inc(S.ro, 1)
 
     P.wait_ge(S.wl, 16)
-    if need_neg:
-        P.wait_ge(S.nws, 1)
-    ready(P, LAST)
-    terms = [(T["v%d" % LAST], sg(LAST, k), None)]
-    terms += [(T["l%d_%d" % (LAST, d)], sg(LAST, k ^ d), d) for d in last_ds]
-    for i, (buf, sig, d) in enumerate(terms):
-        if d is not None:
-            P.wait_ge(S["a%d_%d" % (LAST, d)], n_arr(d))
-        lhs = T.ws[:] if sig > 0 else T.nw[:]
-        for h in range(2):
-            ins = P.matmul(T["py%d" % h][:, 0:HALF], lhs, buf[:, h * HALF:(h + 1) * HALF],
-                           start=(i == 0), stop=(i == len(terms) - 1))
-            if i == len(terms) - 1:
-                ins.then_inc(S["m%d" % h], 1)
-
-    for h, q in enumerate((g.sync, g.scalar)):
-        cols = slice(h * HALF, (h + 1) * HALF)
+    P.wait_ge(S.ro, 1)
+    for h, (q, sem, n, dq) in enumerate(((qn, S.a3, 2 * len(near), g.sync), (qf, S.a4, 2 * len(far), g.scalar))):
+        P.wait_ge(sem, n)
+        P.matmul(T["py%d" % h][:, 0:Q], T.ws[:], quad(T.rs, q), start=True, stop=True).then_inc(S["m%d" % h], 1)
         V.wait_ge(S["m%d" % h], 1)
-        V.tensor_copy(T.yo[:, cols], T["py%d" % h][:, 0:HALF]).then_inc(S["c%d" % h], 1)
-        q.wait_ge(S["c%d" % h], 1)
-        q.dma_start(T.y[:, cols], T.yo[:, cols]).then_inc(S.st, 16)
+        V.tensor_copy(quad(T.yo, q), T["py%d" % h][:, 0:Q]).then_inc(S["c%d" % h], 1)
+        dq.wait_ge(S["c%d" % h], 1)
+        dq.dma_start(quad(T.y, q), quad(T.yo, q)).then_inc(S.st, 16)
 
-    g.wait_ge(S.ls, left)
+    g.wait_ge(S.ls, left[0])
     g.wait_ge(S.st, 32)

@@ -4,13 +4,14 @@ from concourse.mybir import AluOpType
 N = 8
 CH = 64
 Q = 256
+CALLS = (((4, 2), (5, 2), (6, 2), (7, 2)), ((1, 4), (2, 4)), ((3, 8),))
 
 SCRATCH = {
     "xs": ("sbuf", [128, 512], "float32"),
     "la": ("sbuf", [128, 512], "float32"),
     "us0": ("sbuf", [128, 128], "float32"),
     "us1": ("sbuf", [128, 128], "float32"),
-    "vf": ("sbuf", [128, 256], "float32"),
+    "vn": ("sbuf", [128, 256], "float32"),
     "ts": ("sbuf", [128, 512], "float32"),
     "rs": ("sbuf", [128, 512], "float32"),
     "ws": ("sbuf", [128, 128], "float32"),
@@ -20,8 +21,10 @@ SCRATCH = {
     "pv": ("psum", [128, 512], "float32"),
     "py0": ("psum", [128, 512], "float32"),
     "py1": ("psum", [128, 512], "float32"),
+    "py2": ("psum", [128, 512], "float32"),
 }
-SEMAPHORES = ["xn", "xf", "wl", "ls", "st", "a1", "a2", "a3", "a4", "dv", "tn", "tf", "ro", "m0", "m1", "c0", "c1"]
+SEMAPHORES = ["xn", "xf", "wl", "ls", "st", "a10", "a11", "a12", "a20", "a21", "a22", "dv", "tn", "tf", "ro",
+              "m0", "m1", "m2", "c0", "c1", "c2"]
 
 
 def rank_program(g, core, T, topo):
@@ -38,47 +41,45 @@ def rank_program(g, core, T, topo):
     def ch(buf, j):
         return buf[:, j * CH:(j + 1) * CH]
 
+    def pair(buf, j):
+        return buf[:, (j // 2) * 2 * CH:(j // 2 + 1) * 2 * CH]
+
     def quad(buf, q):
         return buf[:, q * Q:(q + 1) * Q]
 
     def op(bit, out_bit):
         return AluOpType.add if sign[bit * out_bit][bit] > 0 else AluOpType.subtract
 
-    near = [j for j in range(N) if j // 4 == qn and j != k]
-    far = [j for j in range(N) if j // 4 == qf]
+    n_call = [sum(n for _, n in call) for call in CALLS]
 
-    def per_transfer(dsts):
-        lists = []
-        for i, j in enumerate(dsts):
-            m = topo.mask(core, T.cores[j])
-            e = [b for b in range(16) if (m >> b) & 1]
-            lists.append((1 << e[2 * i]) | (1 << e[2 * i + 1]))
-        return lists
+    def phase(p, src_buf, dst_buf, go_near, go_far):
+        waited = set()
+        for c, call in enumerate(CALLS):
+            trs, used = [], 0
+            for d, n in call:
+                j = k ^ d
+                go = go_near if d < 4 else go_far
+                if go not in waited:
+                    g.wait_ge(*go)
+                    waited.add(go)
+                m = topo.mask(core, T.cores[j])
+                e = [b for b in range(16) if (m >> b) & 1]
+                e = e[0::2] + e[1::2]
+                rid, pid = topo.addr(T.cores[j], core)
+                trs.append(RemoteDMATransfer(dst_ids=[DstId(rid=rid, pnc=pid)],
+                                             dma_engine_mask=sum(1 << b for b in e[used:used + n]),
+                                             remote_sem=S["a%d%d" % (p, c)],
+                                             src=ch(src_buf, j), dst=ch(dst_buf, k)))
+                used += n
+            g.remote_dma_fused(trs, local_sem=S.ls)
 
-    left = [0]
-
-    def wave(dsts, src_buf, dst_buf, sem):
-        trs = []
-        for j, m in zip(dsts, per_transfer(dsts)):
-            rid, pid = topo.addr(T.cores[j], core)
-            trs.append(RemoteDMATransfer(dst_ids=[DstId(rid=rid, pnc=pid)], dma_engine_mask=m, remote_sem=sem,
-                                         src=ch(src_buf, j), dst=ch(dst_buf, k)))
-            left[0] += 2
-        g.remote_dma_fused(trs, local_sem=S.ls)
-
-    g.sync.dma_start(quad(T.xs, qn), quad(T.x, qn)).then_inc(S.xn, 16)
-    g.scalar.dma_start(quad(T.xs, qf), quad(T.x, qf)).then_inc(S.xf, 16)
-    g.sync.wait_ge(S.xf, 16)
+    g.sync.dma_start(quad(T.xs, qf), quad(T.x, qf)).then_inc(S.xf, 16)
+    g.scalar.dma_start(quad(T.xs, qn), quad(T.x, qn)).then_inc(S.xn, 16)
+    g.sync.wait_ge(S.xn, 16)
     g.sync.dma_start(T.ws[:], T.w[:]).then_inc(S.wl, 16)
 
-    g.wait_ge(S.xn, 16)
-    wave(near, T.xs, T.la, S.a1)
-    g.wait_ge(S.xf, 16)
-    wave(far, T.xs, T.la, S.a2)
-    g.wait_ge(S.tn, 1)
-    wave(near, T.ts, T.rs, S.a3)
-    g.wait_ge(S.tf, 1)
-    wave(far, T.ts, T.rs, S.a4)
+    phase(1, T.xs, T.la, (S.xn, 16), (S.xf, 16))
+    phase(2, T.ts, T.rs, (S.tn, 1), (S.tf, 1))
 
     done = [0]
 
@@ -86,38 +87,58 @@ def rank_program(g, core, T, topo):
         ins.then_inc(S.dv, 1)
         done[0] += 1
 
-    def lower_stages(q, pu, us, out):
-        for b1, dst in ((0, pu), (1, us)):
-            a, b = ch(T.la, 4 * q + 2 * b1), ch(T.la, 4 * q + 2 * b1 + 1)
-            for r0 in range(2):
-                step(V.tensor_tensor(ch(dst, r0), a, b, op(1, r0)))
+    def stage_a(j, pu, us):
+        lo = (j // 2) * 2
+        dst = us if lo & 2 else pu
+        for r0 in range(2):
+            step(V.tensor_tensor(ch(dst, r0), ch(T.la, lo), ch(T.la, lo + 1), op(1, r0)))
+
+    def stage_b(pu, us, out):
         V.wait_ge(S.dv, done[0])
         for r1 in range(2):
             step(V.tensor_tensor(out[:, r1 * 128:(r1 + 1) * 128], pu[:, 0:128], us[:, 0:128], op(2, r1)))
 
     V.wait_ge(S.xn, 16)
     step(V.tensor_copy(ch(T.la, k), ch(T.xs, k)))
-    V.wait_ge(S.a1, 2 * len(near))
+    V.wait_ge(S.a10, n_call[0])
+    stage_a(4 * qf, T.pu0, T.us0)
+    stage_a(4 * qf + 2, T.pu0, T.us0)
+    stage_b(T.pu0, T.us0, T.pv)
+    V.wait_ge(S.a11, n_call[1])
+    stage_a(k, T.pu1, T.us1)
+    V.wait_ge(S.a12, n_call[2])
+    stage_a(k ^ 2, T.pu1, T.us1)
+    stage_b(T.pu1, T.us1, T.vn)
     V.wait_ge(S.dv, done[0])
-    lower_stages(qn, T.pu0, T.us0, T.pv)
-    V.wait_ge(S.a2, 2 * len(far))
-    lower_stages(qf, T.pu1, T.us1, T.vf)
-    V.wait_ge(S.dv, done[0])
-    lo, hi = (T.pv[:, 0:Q], T.vf[:]) if qn == 0 else (T.vf[:], T.pv[:, 0:Q])
-    V.tensor_tensor(quad(T.ts, qn), lo, hi, op(4, qn)).then_inc(S.tn, 1)
+    lo, hi = (T.vn[:], T.pv[:, 0:Q]) if qn == 0 else (T.pv[:, 0:Q], T.vn[:])
     V.tensor_tensor(quad(T.ts, qf), lo, hi, op(4, qf)).then_inc(S.tf, 1)
+    V.tensor_tensor(quad(T.ts, qn), lo, hi, op(4, qn)).then_inc(S.tn, 1)
     V.wait_ge(S.tn, 1)
     V.tensor_copy(ch(T.rs, k), ch(T.ts, k)).then_inc(S.ro, 1)
 
     P.wait_ge(S.wl, 16)
+    P.wait_ge(S.a20, n_call[0])
+    P.matmul(T.py0[:, 0:Q], T.ws[:], quad(T.rs, qf), start=True, stop=True).then_inc(S.m0, 1)
     P.wait_ge(S.ro, 1)
-    for h, (q, sem, n, dq) in enumerate(((qn, S.a3, 2 * len(near), g.sync), (qf, S.a4, 2 * len(far), g.scalar))):
-        P.wait_ge(sem, n)
-        P.matmul(T["py%d" % h][:, 0:Q], T.ws[:], quad(T.rs, q), start=True, stop=True).then_inc(S["m%d" % h], 1)
-        V.wait_ge(S["m%d" % h], 1)
-        V.tensor_copy(quad(T.yo, q), T["py%d" % h][:, 0:Q]).then_inc(S["c%d" % h], 1)
-        dq.wait_ge(S["c%d" % h], 1)
-        dq.dma_start(quad(T.y, q), quad(T.yo, q)).then_inc(S.st, 16)
+    P.wait_ge(S.a21, n_call[1])
+    P.matmul(T.py1[:, 0:128], T.ws[:], pair(T.rs, k), start=True, stop=True).then_inc(S.m1, 1)
+    P.matmul(T.py1[:, 128:192], T.ws[:], ch(T.rs, k ^ 2), start=True, stop=True).then_inc(S.m1, 1)
+    P.wait_ge(S.a22, n_call[2])
+    P.matmul(T.py2[:, 0:CH], T.ws[:], ch(T.rs, k ^ 3), start=True, stop=True).then_inc(S.m2, 1)
 
-    g.wait_ge(S.ls, left[0])
-    g.wait_ge(S.st, 32)
+    V.wait_ge(S.m0, 1)
+    V.tensor_copy(quad(T.yo, qf), T.py0[:, 0:Q]).then_inc(S.c0, 1)
+    V.wait_ge(S.m1, 2)
+    V.tensor_copy(pair(T.yo, k), T.py1[:, 0:128]).then_inc(S.c1, 1)
+    V.tensor_copy(ch(T.yo, k ^ 2), T.py1[:, 128:192]).then_inc(S.c2, 1)
+    V.wait_ge(S.m2, 1)
+    V.tensor_copy(ch(T.yo, k ^ 3), T.py2[:, 0:CH]).then_inc(S.c2, 1)
+    g.sync.wait_ge(S.c0, 1)
+    g.sync.dma_start(quad(T.y, qf), quad(T.yo, qf)).then_inc(S.st, 16)
+    g.scalar.wait_ge(S.c1, 1)
+    g.scalar.dma_start(pair(T.y, k), pair(T.yo, k)).then_inc(S.st, 16)
+    g.sync.wait_ge(S.c2, 2)
+    g.sync.dma_start(pair(T.y, k ^ 2), pair(T.yo, k ^ 2)).then_inc(S.st, 16)
+
+    g.wait_ge(S.ls, 2 * sum(n_call))
+    g.wait_ge(S.st, 48)

@@ -3,28 +3,34 @@ from concourse.mybir import AluOpType
 
 N = 8
 CH = 64
+PR = 128
 Q = 256
-CALLS = (((4, 2), (5, 2), (6, 2), (7, 2)), ((1, 4), (2, 4)), ((3, 8),))
+CALLS = (((4, 4), (5, 4)), ((6, 4), (7, 4)), ((1, 4), (2, 4)), ((3, 8),))
+LAST = 3
 
 SCRATCH = {
     "xs": ("sbuf", [128, 512], "float32"),
     "la": ("sbuf", [128, 512], "float32"),
     "us0": ("sbuf", [128, 128], "float32"),
-    "us1": ("sbuf", [128, 128], "float32"),
-    "vn": ("sbuf", [128, 256], "float32"),
+    "ua": ("sbuf", [128, 128], "float32"),
+    "ub": ("sbuf", [128, 128], "float32"),
     "ts": ("sbuf", [128, 512], "float32"),
     "rs": ("sbuf", [128, 512], "float32"),
     "ws": ("sbuf", [128, 128], "float32"),
+    "wp": ("sbuf", [128, 128], "float32"),
+    "ysd": ("sbuf", [128, 64], "float32"),
     "yo": ("sbuf", [128, 512], "float32"),
     "pu0": ("psum", [128, 512], "float32"),
-    "pu1": ("psum", [128, 512], "float32"),
     "pv": ("psum", [128, 512], "float32"),
-    "py0": ("psum", [128, 512], "float32"),
-    "py1": ("psum", [128, 512], "float32"),
-    "py2": ("psum", [128, 512], "float32"),
+    "pe": ("psum", [128, 512], "float32"),
+    "pyp": ("psum", [128, 512], "float32"),
+    "pyk": ("psum", [128, 512], "float32"),
+    "pya": ("psum", [128, 512], "float32"),
+    "pyb": ("psum", [128, 512], "float32"),
+    "pyc": ("psum", [128, 512], "float32"),
 }
-SEMAPHORES = ["xn", "xf", "wl", "ls", "st", "a10", "a11", "a12", "a20", "a21", "a22", "dv", "tn", "tf", "ro",
-              "m0", "m1", "m2", "c0", "c1", "c2"]
+SEMAPHORES = ["xn", "xf", "wl", "ls", "st", "a10", "a11", "a12", "a13", "a20", "a21", "a22", "a23", "aw", "dv",
+              "t0", "t1", "t2", "t3", "mp", "ma", "mb", "mk", "mc", "yc", "ca", "cb", "ck", "cc"]
 
 
 def rank_program(g, core, T, topo):
@@ -35,51 +41,69 @@ def rank_program(g, core, T, topo):
     S = T.sem
     V = g.vector
     P = g.tensor
+    ADD, SUB = AluOpType.add, AluOpType.subtract
     qn = k // 4
     qf = 1 - qn
+    pk = (k % 4) // 2
+    po = 1 - pk
 
     def ch(buf, j):
         return buf[:, j * CH:(j + 1) * CH]
 
     def pair(buf, j):
-        return buf[:, (j // 2) * 2 * CH:(j // 2 + 1) * 2 * CH]
+        return buf[:, (j // 2) * PR:(j // 2 + 1) * PR]
 
     def quad(buf, q):
         return buf[:, q * Q:(q + 1) * Q]
 
     def op(bit, out_bit):
-        return AluOpType.add if sign[bit * out_bit][bit] > 0 else AluOpType.subtract
+        return ADD if sign[bit * out_bit][bit] > 0 else SUB
+
+    def engines(j):
+        m = topo.mask(core, T.cores[j])
+        e = [b for b in range(16) if (m >> b) & 1]
+        return e[0::2] + e[1::2]
 
     n_call = [sum(n for _, n in call) for call in CALLS]
 
-    def phase(p, src_buf, dst_buf, go_near, go_far):
-        waited = set()
-        for c, call in enumerate(CALLS):
-            trs, used = [], 0
-            for d, n in call:
-                j = k ^ d
-                go = go_near if d < 4 else go_far
-                if go not in waited:
-                    g.wait_ge(*go)
-                    waited.add(go)
-                m = topo.mask(core, T.cores[j])
-                e = [b for b in range(16) if (m >> b) & 1]
-                e = e[0::2] + e[1::2]
-                rid, pid = topo.addr(T.cores[j], core)
-                trs.append(RemoteDMATransfer(dst_ids=[DstId(rid=rid, pnc=pid)],
-                                             dma_engine_mask=sum(1 << b for b in e[used:used + n]),
-                                             remote_sem=S["a%d%d" % (p, c)],
-                                             src=ch(src_buf, j), dst=ch(dst_buf, k)))
-                used += n
-            g.remote_dma_fused(trs, local_sem=S.ls)
+    def call(p, c, src_of, dst_of):
+        trs, used = [], 0
+        for d, n in CALLS[c]:
+            j = k ^ d
+            e = engines(j)
+            rid, pid = topo.addr(T.cores[j], core)
+            trs.append(RemoteDMATransfer(dst_ids=[DstId(rid=rid, pnc=pid)],
+                                         dma_engine_mask=sum(1 << b for b in e[used:used + n]),
+                                         remote_sem=S["a%d%d" % (p, c)],
+                                         src=src_of(j), dst=dst_of(j)))
+            used += n
+        g.remote_dma_fused(trs, local_sem=S.ls)
 
     g.sync.dma_start(quad(T.xs, qf), quad(T.x, qf)).then_inc(S.xf, 16)
     g.scalar.dma_start(quad(T.xs, qn), quad(T.x, qn)).then_inc(S.xn, 16)
     g.sync.wait_ge(S.xn, 16)
     g.sync.dma_start(T.ws[:], T.w[:]).then_inc(S.wl, 16)
 
-    phase(1, T.xs, T.la, (S.xn, 16), (S.xf, 16))
-    phase(2, T.ts, T.rs, (S.tn, 1), (S.tf, 1))
+    g.wait_ge(S.xf, 16)
+    call(1, 0, lambda j: ch(T.xs, j), lambda j: ch(T.la, k))
+    call(1, 1, lambda j: ch(T.xs, j), lambda j: ch(T.la, k))
+    g.wait_ge(S.xn, 16)
+    call(1, 2, lambda j: ch(T.xs, j), lambda j: ch(T.la, k))
+    call(1, 3, lambda j: ch(T.xs, j), lambda j: ch(T.la, k))
+    jl = k ^ LAST
+    n_w = len(engines(jl))
+    rid, pid = topo.addr(T.cores[jl], core)
+    g.wait_ge(S.wl, 16)
+    g.remote_dma(T.wp[:], T.ws[:], S.aw, S.ls, pid, rid, topo.mask(core, T.cores[jl]))
+    g.wait_ge(S.t0, 1)
+    call(2, 0, lambda j: ch(T.ts, j), lambda j: ch(T.rs, k))
+    g.wait_ge(S.t1, 1)
+    call(2, 1, lambda j: ch(T.ts, j), lambda j: ch(T.rs, k))
+    g.wait_ge(S.t2, 1)
+    g.wait_ge(S.t3, 1)
+    call(2, 2, lambda j: ch(T.ts, j), lambda j: ch(T.rs, k))
+    g.wait_ge(S.yc, 1)
+    call(2, 3, lambda j: T.ysd[:], lambda j: ch(T.yo, k))
 
     done = [0]
 
@@ -87,58 +111,105 @@ def rank_program(g, core, T, topo):
         ins.then_inc(S.dv, 1)
         done[0] += 1
 
-    def stage_a(j, pu, us):
-        lo = (j // 2) * 2
-        dst = us if lo & 2 else pu
-        for r0 in range(2):
-            step(V.tensor_tensor(ch(dst, r0), ch(T.la, lo), ch(T.la, lo + 1), op(1, r0)))
-
-    def stage_b(pu, us, out):
+    def settle():
         V.wait_ge(S.dv, done[0])
-        for r1 in range(2):
-            step(V.tensor_tensor(out[:, r1 * 128:(r1 + 1) * 128], pu[:, 0:128], us[:, 0:128], op(2, r1)))
 
-    V.wait_ge(S.xn, 16)
-    step(V.tensor_copy(ch(T.la, k), ch(T.xs, k)))
+    def src(j):
+        return ch(T.xs, k) if j == k else ch(T.la, j)
+
+    def stage_a(j, dst):
+        lo = (j // 2) * 2
+        for r0 in range(2):
+            step(V.tensor_tensor(ch(dst, r0), src(lo), src(lo + 1), op(1, r0)))
+
+    a0 = (k // 2) * 2
+    b0 = ((k ^ 2) // 2) * 2
+    fb = 4 * qf
+
+    def e_of(q, r1):
+        return T.pe[:, (2 * q + r1) * PR:(2 * q + r1 + 1) * PR]
+
+    def bracket(q, r1):
+        s_a, s_f = sign[4 * q + 2 * r1][a0], sign[4 * q + 2 * r1][fb]
+        v_f = T.pv[:, r1 * PR:(r1 + 1) * PR]
+        if s_a > 0:
+            step(V.tensor_tensor(e_of(q, r1), T.ua[:], v_f, ADD if s_f > 0 else SUB))
+            return 1
+        if s_f > 0:
+            step(V.tensor_tensor(e_of(q, r1), v_f, T.ua[:], SUB))
+            return 1
+        step(V.tensor_tensor(e_of(q, r1), T.ua[:], v_f, ADD))
+        return -1
+
+    def finish(q, r1, s_e, sem):
+        s_b = sign[4 * q + 2 * r1][b0]
+        out = T.ts[:, q * Q + r1 * PR:q * Q + (r1 + 1) * PR]
+        if s_e > 0:
+            V.tensor_tensor(out, e_of(q, r1), T.ub[:], ADD if s_b > 0 else SUB).then_inc(sem, 1)
+        else:
+            assert s_b > 0
+            V.tensor_tensor(out, T.ub[:], e_of(q, r1), SUB).then_inc(sem, 1)
+
+    def far_dst(j):
+        return T.us0 if j & 2 else T.pu0
+
     V.wait_ge(S.a10, n_call[0])
-    stage_a(4 * qf, T.pu0, T.us0)
-    stage_a(4 * qf + 2, T.pu0, T.us0)
-    stage_b(T.pu0, T.us0, T.pv)
+    stage_a(k ^ 4, far_dst(k ^ 4))
     V.wait_ge(S.a11, n_call[1])
-    stage_a(k, T.pu1, T.us1)
+    stage_a(k ^ 6, far_dst(k ^ 6))
+    settle()
+    for r1 in range(2):
+        step(V.tensor_tensor(T.pv[:, r1 * PR:(r1 + 1) * PR], T.pu0[:, 0:PR], T.us0[:], op(2, r1)))
+    V.wait_ge(S.xn, 16)
     V.wait_ge(S.a12, n_call[2])
-    stage_a(k ^ 2, T.pu1, T.us1)
-    stage_b(T.pu1, T.us1, T.vn)
-    V.wait_ge(S.dv, done[0])
-    lo, hi = (T.vn[:], T.pv[:, 0:Q]) if qn == 0 else (T.pv[:, 0:Q], T.vn[:])
-    V.tensor_tensor(quad(T.ts, qf), lo, hi, op(4, qf)).then_inc(S.tf, 1)
-    V.tensor_tensor(quad(T.ts, qn), lo, hi, op(4, qn)).then_inc(S.tn, 1)
-    V.wait_ge(S.tn, 1)
-    V.tensor_copy(ch(T.rs, k), ch(T.ts, k)).then_inc(S.ro, 1)
+    stage_a(k, T.ua)
+    settle()
+    e0 = bracket(qf, pk)
+    e1 = bracket(qf, po)
+    V.wait_ge(S.a13, n_call[3])
+    stage_a(k ^ 2, T.ub)
+    settle()
+    finish(qf, pk, e0, S.t0)
+    finish(qf, po, e1, S.t1)
+    e2 = bracket(qn, po)
+    e3 = bracket(qn, pk)
+    settle()
+    finish(qn, po, e2, S.t2)
+    finish(qn, pk, e3, S.t3)
 
+    P.wait_ge(S.aw, n_w)
+    P.wait_ge(S.t2, 1)
+    P.matmul(T.pyp[:, 0:CH], T.wp[:], ch(T.ts, jl), start=True, stop=True).then_inc(S.mp, 1)
     P.wait_ge(S.wl, 16)
+    P.wait_ge(S.t3, 1)
+    P.matmul(ch(T.pyk, k % 2), T.ws[:], ch(T.ts, k), start=True, stop=True).then_inc(S.mk, 1)
     P.wait_ge(S.a20, n_call[0])
-    P.matmul(T.py0[:, 0:Q], T.ws[:], quad(T.rs, qf), start=True, stop=True).then_inc(S.m0, 1)
-    P.wait_ge(S.ro, 1)
+    P.matmul(T.pya[:, 0:PR], T.ws[:], pair(T.rs, k ^ 4), start=True, stop=True).then_inc(S.ma, 1)
     P.wait_ge(S.a21, n_call[1])
-    P.matmul(T.py1[:, 0:128], T.ws[:], pair(T.rs, k), start=True, stop=True).then_inc(S.m1, 1)
-    P.matmul(T.py1[:, 128:192], T.ws[:], ch(T.rs, k ^ 2), start=True, stop=True).then_inc(S.m1, 1)
+    P.matmul(T.pyb[:, 0:PR], T.ws[:], pair(T.rs, k ^ 6), start=True, stop=True).then_inc(S.mb, 1)
     P.wait_ge(S.a22, n_call[2])
-    P.matmul(T.py2[:, 0:CH], T.ws[:], ch(T.rs, k ^ 3), start=True, stop=True).then_inc(S.m2, 1)
+    P.matmul(ch(T.pyk, (k ^ 1) % 2), T.ws[:], ch(T.rs, k ^ 1), start=True, stop=True).then_inc(S.mk, 1)
+    P.matmul(T.pyc[:, 0:CH], T.ws[:], ch(T.rs, k ^ 2), start=True, stop=True).then_inc(S.mc, 1)
 
-    V.wait_ge(S.m0, 1)
-    V.tensor_copy(quad(T.yo, qf), T.py0[:, 0:Q]).then_inc(S.c0, 1)
-    V.wait_ge(S.m1, 2)
-    V.tensor_copy(pair(T.yo, k), T.py1[:, 0:128]).then_inc(S.c1, 1)
-    V.tensor_copy(ch(T.yo, k ^ 2), T.py1[:, 128:192]).then_inc(S.c2, 1)
-    V.wait_ge(S.m2, 1)
-    V.tensor_copy(ch(T.yo, k ^ 3), T.py2[:, 0:CH]).then_inc(S.c2, 1)
-    g.sync.wait_ge(S.c0, 1)
-    g.sync.dma_start(quad(T.y, qf), quad(T.yo, qf)).then_inc(S.st, 16)
-    g.scalar.wait_ge(S.c1, 1)
-    g.scalar.dma_start(pair(T.y, k), pair(T.yo, k)).then_inc(S.st, 16)
-    g.sync.wait_ge(S.c2, 2)
-    g.sync.dma_start(pair(T.y, k ^ 2), pair(T.yo, k ^ 2)).then_inc(S.st, 16)
+    V.wait_ge(S.mp, 1)
+    V.tensor_copy(T.ysd[:], T.pyp[:, 0:CH]).then_inc(S.yc, 1)
+    V.wait_ge(S.ma, 1)
+    V.tensor_copy(pair(T.yo, k ^ 4), T.pya[:, 0:PR]).then_inc(S.ca, 1)
+    V.wait_ge(S.mb, 1)
+    V.tensor_copy(pair(T.yo, k ^ 6), T.pyb[:, 0:PR]).then_inc(S.cb, 1)
+    V.wait_ge(S.mk, 2)
+    V.tensor_copy(pair(T.yo, k), T.pyk[:, 0:PR]).then_inc(S.ck, 1)
+    V.wait_ge(S.mc, 1)
+    V.tensor_copy(ch(T.yo, k ^ 2), T.pyc[:, 0:CH]).then_inc(S.cc, 1)
+    g.sync.wait_ge(S.ca, 1)
+    g.sync.dma_start(pair(T.y, k ^ 4), pair(T.yo, k ^ 4)).then_inc(S.st, 16)
+    g.scalar.wait_ge(S.cb, 1)
+    g.scalar.dma_start(pair(T.y, k ^ 6), pair(T.yo, k ^ 6)).then_inc(S.st, 16)
+    g.sync.wait_ge(S.ck, 1)
+    g.sync.dma_start(pair(T.y, k), pair(T.yo, k)).then_inc(S.st, 16)
+    g.scalar.wait_ge(S.cc, 1)
+    g.scalar.wait_ge(S.a23, n_call[3])
+    g.scalar.dma_start(pair(T.y, k ^ 2), pair(T.yo, k ^ 2)).then_inc(S.st, 16)
 
-    g.wait_ge(S.ls, 2 * sum(n_call))
-    g.wait_ge(S.st, 48)
+    g.wait_ge(S.ls, 2 * sum(n_call) + n_w)
+    g.wait_ge(S.st, 64)

from concourse.bass import DstId, RemoteDMATransfer
from concourse.mybir import AluOpType

N = 8
CH = 64
PR = 128
Q = 256
CALLS = (((4, 4), (5, 4)), ((6, 4), (7, 4)), ((1, 4), (2, 4)), ((3, 8),))
LAST = 3

SCRATCH = {
    "xs": ("sbuf", [128, 512], "float32"),
    "la": ("sbuf", [128, 512], "float32"),
    "us0": ("sbuf", [128, 128], "float32"),
    "ua": ("sbuf", [128, 128], "float32"),
    "ub": ("sbuf", [128, 128], "float32"),
    "ts": ("sbuf", [128, 512], "float32"),
    "rs": ("sbuf", [128, 512], "float32"),
    "ws": ("sbuf", [128, 128], "float32"),
    "wp": ("sbuf", [128, 128], "float32"),
    "ysd": ("sbuf", [128, 64], "float32"),
    "yo": ("sbuf", [128, 512], "float32"),
    "pu0": ("psum", [128, 512], "float32"),
    "pv": ("psum", [128, 512], "float32"),
    "pe": ("psum", [128, 512], "float32"),
    "pyp": ("psum", [128, 512], "float32"),
    "pyk": ("psum", [128, 512], "float32"),
    "pya": ("psum", [128, 512], "float32"),
    "pyb": ("psum", [128, 512], "float32"),
    "pyc": ("psum", [128, 512], "float32"),
}
SEMAPHORES = ["xn", "xf", "wl", "ls", "st", "a10", "a11", "a12", "a13", "a20", "a21", "a22", "a23", "aw", "dv",
              "t0", "t1", "t2", "t3", "mp", "ma", "mb", "mk", "mc", "yc", "ca", "cb", "ck", "cc"]


def rank_program(g, core, T, topo):
    k = T.rank_of(core)
    if k is None:
        return
    sign = T.tables["SIGN"]
    S = T.sem
    V = g.vector
    P = g.tensor
    ADD, SUB = AluOpType.add, AluOpType.subtract
    qn = k // 4
    qf = 1 - qn
    pk = (k % 4) // 2
    po = 1 - pk

    def ch(buf, j):
        return buf[:, j * CH:(j + 1) * CH]

    def pair(buf, j):
        return buf[:, (j // 2) * PR:(j // 2 + 1) * PR]

    def quad(buf, q):
        return buf[:, q * Q:(q + 1) * Q]

    def op(bit, out_bit):
        return ADD if sign[bit * out_bit][bit] > 0 else SUB

    def engines(j):
        m = topo.mask(core, T.cores[j])
        e = [b for b in range(16) if (m >> b) & 1]
        return e[0::2] + e[1::2]

    n_call = [sum(n for _, n in call) for call in CALLS]

    def call(p, c, src_of, dst_of):
        trs, used = [], 0
        for d, n in CALLS[c]:
            j = k ^ d
            e = engines(j)
            rid, pid = topo.addr(T.cores[j], core)
            trs.append(RemoteDMATransfer(dst_ids=[DstId(rid=rid, pnc=pid)],
                                         dma_engine_mask=sum(1 << b for b in e[used:used + n]),
                                         remote_sem=S["a%d%d" % (p, c)],
                                         src=src_of(j), dst=dst_of(j)))
            used += n
        g.remote_dma_fused(trs, local_sem=S.ls)

    g.sync.dma_start(quad(T.xs, qf), quad(T.x, qf)).then_inc(S.xf, 16)
    g.scalar.dma_start(quad(T.xs, qn), quad(T.x, qn)).then_inc(S.xn, 16)
    g.sync.wait_ge(S.xn, 16)
    g.sync.dma_start(T.ws[:], T.w[:]).then_inc(S.wl, 16)

    g.wait_ge(S.xf, 16)
    call(1, 0, lambda j: ch(T.xs, j), lambda j: ch(T.la, k))
    call(1, 1, lambda j: ch(T.xs, j), lambda j: ch(T.la, k))
    g.wait_ge(S.xn, 16)
    call(1, 2, lambda j: ch(T.xs, j), lambda j: ch(T.la, k))
    call(1, 3, lambda j: ch(T.xs, j), lambda j: ch(T.la, k))
    jl = k ^ LAST
    n_w = len(engines(jl))
    rid, pid = topo.addr(T.cores[jl], core)
    g.wait_ge(S.wl, 16)
    g.remote_dma(T.wp[:], T.ws[:], S.aw, S.ls, pid, rid, topo.mask(core, T.cores[jl]))
    g.wait_ge(S.t0, 1)
    call(2, 0, lambda j: ch(T.ts, j), lambda j: ch(T.rs, k))
    g.wait_ge(S.t1, 1)
    call(2, 1, lambda j: ch(T.ts, j), lambda j: ch(T.rs, k))
    g.wait_ge(S.t2, 1)
    g.wait_ge(S.t3, 1)
    call(2, 2, lambda j: ch(T.ts, j), lambda j: ch(T.rs, k))
    g.wait_ge(S.yc, 1)
    call(2, 3, lambda j: T.ysd[:], lambda j: ch(T.yo, k))

    done = [0]

    def step(ins):
        ins.then_inc(S.dv, 1)
        done[0] += 1

    def settle():
        V.wait_ge(S.dv, done[0])

    def src(j):
        return ch(T.xs, k) if j == k else ch(T.la, j)

    def stage_a(j, dst):
        lo = (j // 2) * 2
        for r0 in range(2):
            step(V.tensor_tensor(ch(dst, r0), src(lo), src(lo + 1), op(1, r0)))

    a0 = (k // 2) * 2
    b0 = ((k ^ 2) // 2) * 2
    fb = 4 * qf

    def e_of(q, r1):
        return T.pe[:, (2 * q + r1) * PR:(2 * q + r1 + 1) * PR]

    def bracket(q, r1):
        s_a, s_f = sign[4 * q + 2 * r1][a0], sign[4 * q + 2 * r1][fb]
        v_f = T.pv[:, r1 * PR:(r1 + 1) * PR]
        if s_a > 0:
            step(V.tensor_tensor(e_of(q, r1), T.ua[:], v_f, ADD if s_f > 0 else SUB))
            return 1
        if s_f > 0:
            step(V.tensor_tensor(e_of(q, r1), v_f, T.ua[:], SUB))
            return 1
        step(V.tensor_tensor(e_of(q, r1), T.ua[:], v_f, ADD))
        return -1

    def finish(q, r1, s_e, sem):
        s_b = sign[4 * q + 2 * r1][b0]
        out = T.ts[:, q * Q + r1 * PR:q * Q + (r1 + 1) * PR]
        if s_e > 0:
            V.tensor_tensor(out, e_of(q, r1), T.ub[:], ADD if s_b > 0 else SUB).then_inc(sem, 1)
        else:
            assert s_b > 0
            V.tensor_tensor(out, T.ub[:], e_of(q, r1), SUB).then_inc(sem, 1)

    def far_dst(j):
        return T.us0 if j & 2 else T.pu0

    V.wait_ge(S.a10, n_call[0])
    stage_a(k ^ 4, far_dst(k ^ 4))
    V.wait_ge(S.a11, n_call[1])
    stage_a(k ^ 6, far_dst(k ^ 6))
    settle()
    for r1 in range(2):
        step(V.tensor_tensor(T.pv[:, r1 * PR:(r1 + 1) * PR], T.pu0[:, 0:PR], T.us0[:], op(2, r1)))
    V.wait_ge(S.xn, 16)
    V.wait_ge(S.a12, n_call[2])
    stage_a(k, T.ua)
    settle()
    e0 = bracket(qf, pk)
    e1 = bracket(qf, po)
    V.wait_ge(S.a13, n_call[3])
    stage_a(k ^ 2, T.ub)
    settle()
    finish(qf, pk, e0, S.t0)
    finish(qf, po, e1, S.t1)
    e2 = bracket(qn, po)
    e3 = bracket(qn, pk)
    settle()
    finish(qn, po, e2, S.t2)
    finish(qn, pk, e3, S.t3)

    P.wait_ge(S.aw, n_w)
    P.wait_ge(S.t2, 1)
    P.matmul(T.pyp[:, 0:CH], T.wp[:], ch(T.ts, jl), start=True, stop=True).then_inc(S.mp, 1)
    P.wait_ge(S.wl, 16)
    P.wait_ge(S.t3, 1)
    P.matmul(ch(T.pyk, k % 2), T.ws[:], ch(T.ts, k), start=True, stop=True).then_inc(S.mk, 1)
    P.wait_ge(S.a20, n_call[0])
    P.matmul(T.pya[:, 0:PR], T.ws[:], pair(T.rs, k ^ 4), start=True, stop=True).then_inc(S.ma, 1)
    P.wait_ge(S.a21, n_call[1])
    P.matmul(T.pyb[:, 0:PR], T.ws[:], pair(T.rs, k ^ 6), start=True, stop=True).then_inc(S.mb, 1)
    P.wait_ge(S.a22, n_call[2])
    P.matmul(ch(T.pyk, (k ^ 1) % 2), T.ws[:], ch(T.rs, k ^ 1), start=True, stop=True).then_inc(S.mk, 1)
    P.matmul(T.pyc[:, 0:CH], T.ws[:], ch(T.rs, k ^ 2), start=True, stop=True).then_inc(S.mc, 1)

    V.wait_ge(S.mp, 1)
    V.tensor_copy(T.ysd[:], T.pyp[:, 0:CH]).then_inc(S.yc, 1)
    V.wait_ge(S.ma, 1)
    V.tensor_copy(pair(T.yo, k ^ 4), T.pya[:, 0:PR]).then_inc(S.ca, 1)
    V.wait_ge(S.mb, 1)
    V.tensor_copy(pair(T.yo, k ^ 6), T.pyb[:, 0:PR]).then_inc(S.cb, 1)
    V.wait_ge(S.mk, 2)
    V.tensor_copy(pair(T.yo, k), T.pyk[:, 0:PR]).then_inc(S.ck, 1)
    V.wait_ge(S.mc, 1)
    V.tensor_copy(ch(T.yo, k ^ 2), T.pyc[:, 0:CH]).then_inc(S.cc, 1)
    g.sync.wait_ge(S.ca, 1)
    g.sync.dma_start(pair(T.y, k ^ 4), pair(T.yo, k ^ 4)).then_inc(S.st, 16)
    g.scalar.wait_ge(S.cb, 1)
    g.scalar.dma_start(pair(T.y, k ^ 6), pair(T.yo, k ^ 6)).then_inc(S.st, 16)
    g.sync.wait_ge(S.ck, 1)
    g.sync.dma_start(pair(T.y, k), pair(T.yo, k)).then_inc(S.st, 16)
    g.scalar.wait_ge(S.cc, 1)
    g.scalar.wait_ge(S.a23, n_call[3])
    g.scalar.dma_start(pair(T.y, k ^ 2), pair(T.yo, k ^ 2)).then_inc(S.st, 16)

    g.wait_ge(S.ls, 2 * sum(n_call) + n_w)
    g.wait_ge(S.st, 64)
